import numpy as np
import ml_dtypes


def mxq(x, axis, fmt="e4m3"):
    dtype, down = {"e4m3": (ml_dtypes.float8_e4m3fn, 7), "e5m2": (ml_dtypes.float8_e5m2, 14)}[fmt]
    v = np.moveaxis(np.asarray(x, np.float32).astype(ml_dtypes.bfloat16).astype(np.float64), axis, -1)
    blocks = v.reshape(v.shape[:-1] + (-1, 32))
    amax = np.abs(blocks).max(-1, keepdims=True)
    byte = np.maximum(np.where(amax > 0, np.frexp(amax)[1] - 1 + 127, 0) - down, 1)
    scale = np.exp2(byte - 127.0)
    codes = (blocks / scale).astype(np.float32).astype(dtype).astype(np.float64)
    return np.moveaxis((codes * scale).reshape(v.shape), -1, axis)


WIDE = False


def mx_kscale(k):
    if not WIDE:
        return np.ones(k)
    levels = np.array([10, -10, 5, -5, 0])
    if k % 512:
        return np.exp2(np.random.permutation(np.resize(levels, k // 32))).repeat(32)
    a = np.empty((k // 512, 16))
    for p in range(k // 512):
        a[p, :8] = np.random.permutation(np.resize(levels, 8))
        for g in range(8):
            far = levels[np.abs(levels - a[p, g]) >= 10]
            a[p, g + 8] = far[np.random.randint(len(far))]
    return np.exp2(a.ravel()).repeat(32)


def f64(x):
    return np.asarray(x).astype(np.float64)


def striped(idx):
    return np.tile(idx.reshape(-1, 16).T, (8, 1)).astype(np.uint16)


def unstriped(offs):
    return offs[:16].T.reshape(-1).astype(np.int64)


E2M1 = np.array([0.0, 0.5, 1.0, 1.5, 2.0, 3.0, 4.0, 6.0, -0.0, -0.5, -1.0, -1.5, -2.0, -3.0, -4.0, -6.0])


def pack_weight(w, fmt):
    k, n = w.shape
    w = f64(np.asarray(w, np.float32).astype(ml_dtypes.bfloat16)).reshape(k // 32, 32, n)
    amax = np.abs(w).max(1)
    if fmt == "e4m3":
        byte = np.frexp(amax)[1] - 1 + 127 - 7
    else:
        mant, ex = np.frexp(amax / 6.0)
        byte = np.where(mant > 0.5, ex, ex - 1) + 127
    byte = np.clip(np.where(amax > 0, byte, 1), 1, 254)
    scaled = (w * np.exp2(127.0 - byte)[:, None, :]).reshape(k, n).astype(np.float32)
    by_word = np.ascontiguousarray(scaled.reshape(k // 512, 128, 4, n).transpose(0, 1, 3, 2))
    if fmt == "e4m3":
        words = by_word.astype(ml_dtypes.float8_e4m3fn).view(np.uint8)
    else:
        c = by_word.astype(ml_dtypes.float4_e2m1fn).view(np.uint8) & 0xF
        words = (c[..., 0::2] | (c[..., 1::2] << 4)).reshape(k // 512, 128, 2 * n)
    return np.ascontiguousarray(words), np.ascontiguousarray(byte.astype(np.uint8).reshape(k // 512, 16, n))


def unpack_weight(words, scales, fmt):
    g, _, n = scales.shape
    words = np.ascontiguousarray(words).reshape(g, 128, n, -1)
    if fmt == "e4m3":
        vals = words.view(ml_dtypes.float8_e4m3fn).astype(np.float64)
    else:
        nib = np.empty((g, 128, n, 4), np.uint8)
        nib[..., 0::2] = words & 0xF
        nib[..., 1::2] = words >> 4
        vals = E2M1[nib]
    vals = vals * np.repeat(np.exp2(scales.astype(np.float64) - 127.0), 8, axis=1)[..., None]
    return vals.transpose(0, 1, 3, 2).reshape(g * 512, n)


def gelu(v):
    return 0.5 * v * (1.0 + np.tanh(np.sqrt(2.0 / np.pi) * (v + 0.044715 * v**3)))


K, T, S, H, P, N = 1536, 4096, 1024, 1024, 512, 512

def setup_inputs():
    n = np.random.standard_normal
    s = mx_kscale(K)[:, None]
    u = mx_kscale(H)[:, None]
    d = {}
    d["tab_words"], d["tab_scales"] = pack_weight(n((K, T)) * s, "e2m1")
    d["offs"] = striped(np.random.permutation(T)[:S])
    d["pos1"] = striped(np.random.permutation(S)[:P])
    d["pos2"] = striped(np.random.permutation(S)[:P])
    d["w1"] = (1.3 * n((K, H)) / K**0.5 / s).astype(np.float32)
    d["gain"] = (np.exp(0.4 * n(H)) * u[:, 0]).astype(np.float32)
    d["w2_words"], d["w2_scales"] = pack_weight(n((H, N)) / H**0.5 / u, "e2m1")
    d["w3"] = (1.2 * n((H, N)) / H**0.5 / u).astype(np.float32)
    d["b3"] = (0.5 * n(N)).astype(np.float32)
    return d

def reference(tab_words, tab_scales, offs, pos1, pos2, w1, gain, w2_words, w2_scales, w3, b3):
    v = unpack_weight(tab_words, tab_scales, "e2m1")[:, unstriped(offs)]
    h = np.tanh(mxq(f64(w1), 0, "e4m3").T @ v) * f64(gain)[:, None]
    left = h[:, unstriped(pos1)]
    right = h[:, unstriped(pos2)]
    apart = mxq(left - right, 0, "e4m3")
    joint = mxq(left + right, 0, "e4m3")
    w2 = unpack_weight(w2_words, w2_scales, "e2m1")
    e = w2.T @ apart
    f = (mxq(f64(w3), 0, "e4m3").T @ joint) + f64(b3)[:, None]
    out = np.maximum(np.abs(e), f)
    return out

@@ -1,0 +1,294 @@
+from contextlib import ExitStack
+
+import concourse.mybir as mybir
+
+K, T, S, H, PAIRS, N = 1536, 4096, 1024, 1024, 512, 512
+FLOPS = 2 * K * H * S + 2 * 2 * H * N * PAIRS
+
+F32 = mybir.dt.float32
+BF16 = mybir.dt.bfloat16
+I32 = mybir.dt.int32
+U32 = mybir.dt.uint32
+U16 = mybir.dt.uint16
+U8 = mybir.dt.uint8
+FP8X4 = mybir.dt.float8_e4m3fn_x4
+FP4X4 = mybir.dt.float4_e2m1fn_x4
+ALU = mybir.AluOpType
+ACT = mybir.ActivationFunctionType
+
+P = 128
+PACK = 4
+K_PASS = P * PACK
+BANK = 512
+PASSES1 = K // K_PASS
+PASSES2 = H // K_PASS
+QUADS = 4
+FIRST_ROW = 32 - 4 * PASSES1
+MOVED = 100
+
+
+def tile_list_bone_pair_separation_kernel(
+    tc, tab_words, tab_scales, offs, pos1, pos2, w1, gain, w2_words, w2_scales, w3, b3, out
+):
+    nc = tc.nc
+    with ExitStack() as ctx:
+        keep = ctx.enter_context(tc.tile_pool(name="keep", bufs=1))
+        ring = ctx.enter_context(tc.tile_pool(name="ring", bufs=2))
+        psum = ctx.enter_context(tc.psum_pool(name="psum", bufs=8))
+
+        def held(shape, dtype, name):
+            return keep.tile(shape, dtype, name=name, align_bytes=64)
+
+        def turned(shape, dtype, name, bufs):
+            return ring.tile(shape, dtype, name=name, align_bytes=64, bufs=bufs)
+
+        offs_sb = keep.tile([P, S // 16], U16, name="offs_sb")
+        pos1_sb = keep.tile([P, PAIRS // 16], U16, name="pos1_sb")
+        pos2_sb = keep.tile([P, PAIRS // 16], U16, name="pos2_sb")
+
+        tab_scale = held([P, T], U8, "tab_scale")
+        for q in range(QUADS):
+            (nc.vector if q % 2 else nc.gpsimd).memset(tab_scale[32 * q : 32 * q + FIRST_ROW, :].bitcast(I32), 0)
+        picked_scale = held([P, S], U8, "picked_scale")
+        v_scale = [held([P, S], U8, "v_scale%d" % a) for a in range(PASSES1)]
+        for a in range(PASSES1):
+            nc.vector.memset(v_scale[a][:].bitcast(I32), 0)
+
+        def slot(shape, dtype, tag):
+            return keep.tile(shape, dtype, name=tag, align_bytes=64)
+
+        def load_w(w, row0, col0, width, tag):
+            raw = slot([P, PACK, width], F32, tag)
+            nc.sync.dma_start(
+                raw[:], w[row0 : row0 + K_PASS, col0 : col0 + width].rearrange("(p j) c -> p j c", j=PACK)
+            )
+            return raw
+
+        def load_words(a):
+            words = slot([P, T], U16, "words%d" % a)
+            nc.sync.dma_start(words[:].bitcast(I32), tab_words[a].bitcast(I32))
+            return words
+
+        def load_scale_rows(quads):
+            for a in range(PASSES1):
+                for q in quads:
+                    row = 32 * q + FIRST_ROW + 4 * a
+                    nc.sync.dma_start(
+                        tab_scale[row : row + 4, :].bitcast(I32),
+                        tab_scales[a, 4 * q : 4 * q + 4, :].bitcast(I32),
+                    )
+
+        nc.sync.dma_start(offs_sb[:], offs)
+        load_scale_rows([0, 2])
+        tab_word = [load_words(0)]
+        load_scale_rows([1, 3])
+        w1_raw = {}
+        half = K_PASS // 2
+        for a in range(PASSES1 - 1):
+            w1_raw[0, a] = [load_w(w1, a * K_PASS, 0, K_PASS, "rows%d" % a)]
+            tab_word.append(load_words(a + 1))
+        w1_raw[0, 2] = [load_w(w1, 2 * K_PASS, u * half, half, "half%d" % u) for u in range(2)]
+        nc.sync.dma_start(pos1_sb[:], pos1)
+        nc.sync.dma_start(pos2_sb[:], pos2)
+        gain_sb = held([P, PASSES2, PACK], F32, "gain_sb")
+        nc.gpsimd.dma_start(gain_sb[:], gain.rearrange("(b p t) -> p b t", p=P, t=PACK))
+
+        v_word = [held([P, S], U16, "v_word%d" % a) for a in range(PASSES1)]
+
+        def gather_words(a):
+            nc.vector.tensor_copy(v_word[a][:], tab_word[a][:].indirect(offs_sb[:]))
+
+        def gather_scales():
+            nc.vector.tensor_copy(picked_scale[:], tab_scale[:].indirect(offs_sb[:]))
+            for a in range(PASSES1):
+                row = FIRST_ROW + 4 * a
+                nc.gpsimd.dma_start(
+                    v_scale[a][0:MOVED, :].bitcast(I32), picked_scale[row : row + MOVED, :].bitcast(I32)
+                )
+
+        def copy_on(engine, dst, src):
+            if engine is nc.scalar:
+                nc.scalar.copy(dst, src)
+            else:
+                engine.tensor_copy(dst, src)
+
+        def quantise(grouped, name, pieces):
+            words = K_PASS
+            codes = held([P, words], U32, name + "_codes")
+            scales = held([P, words], U8, name + "_scales")
+            w = words // pieces
+            for i in range(pieces):
+                nc.vector.quantize_mx(
+                    out=codes[:, i * w : (i + 1) * w].bitcast(FP8X4),
+                    scales=scales[:, i * w : (i + 1) * w],
+                    in_=grouped[:, PACK * i * w : PACK * (i + 1) * w],
+                )
+            return codes, scales
+
+        def round_w1(b, a, engines, grouped):
+            view = grouped.rearrange("p (t m j) -> p m j t", t=PACK, j=PACK)
+            parts = w1_raw[b, a]
+            m = P // len(parts)
+            for u, raw in enumerate(parts):
+                copy_on(engines[u], view[:, u * m : (u + 1) * m], raw[:].rearrange("p j (m t) -> p m j t", t=PACK))
+            return grouped
+
+        def round_w3(b, tag):
+            grouped = slot([P, PACK * N], BF16, tag)[:]
+            dst = grouped.rearrange("p (c i j) -> p c j i", i=4, j=PACK)
+            src = w3_raw[b][:].rearrange("p j (c i) -> p c j i", i=4)
+            for u in range(2):
+                nc.scalar.copy(dst[:, 64 * u : 64 * (u + 1)], src[:, 64 * u : 64 * (u + 1)])
+            return grouped
+
+        w1_q = {}
+
+        def first_pass(bank, b, t, a, u):
+            codes, scales = w1_q[b, a]
+            nc.tensor.matmul_mx(
+                out=bank[:],
+                lhsT=codes[:, t * P : (t + 1) * P].bitcast(FP8X4),
+                lhsT_scale=scales[:, t * P : (t + 1) * P],
+                rhs=v_word[a][:, u * BANK : (u + 1) * BANK].bitcast(FP4X4),
+                rhs_scale=v_scale[a][:, u * BANK : (u + 1) * BANK],
+                start=(a == 0),
+                stop=(a == PASSES1 - 1),
+            )
+
+        def reading(banks, b, t, gain_engine, tag):
+            tanh = slot([P, S], F32, tag)
+            for u in range(2):
+                nc.scalar.activation(tanh[:, u * BANK : (u + 1) * BANK], banks[u][:], ACT.Tanh)
+            h = turned([P, S], F32, "h", 4)
+            g = gain_sb[:, b, t : t + 1]
+            if gain_engine is nc.scalar:
+                nc.scalar.activation(h[:], tanh[:], ACT.Copy, scale=g)
+            else:
+                for u in range(2):
+                    cols = slice(u * BANK, (u + 1) * BANK)
+                    nc.vector.tensor_scalar(h[:, cols], tanh[:, cols], g, None, ALU.mult)
+            return h
+
+        def pick(h, left, right, t):
+            nc.vector.tensor_copy(left[:, t, :], h[:].indirect(pos1_sb[:]))
+            nc.vector.tensor_copy(right[:, t, :], h[:].indirect(pos2_sb[:]))
+
+        def combine(left, right, op, tag):
+            grouped = slot([P, PACK * PAIRS], BF16, tag)[:]
+            nc.vector.tensor_tensor(
+                grouped.rearrange("p (c i t) -> p c t i", i=4, t=PACK),
+                left[:].rearrange("p t (c i) -> p c t i", i=4),
+                right[:].rearrange("p t (c i) -> p c t i", i=4),
+                op,
+            )
+            return grouped
+
+        gather_words(0)
+        gather_scales()
+        banks0 = [[psum.tile([P, BANK], F32, name="bank") for u in range(2)] for t in range(PACK)]
+        for a in range(PASSES1):
+            last = a == PASSES1 - 1
+            if a > 0:
+                gather_words(a)
+            grouped = round_w1(0, a, [nc.scalar, nc.vector], slot([P, PACK * K_PASS], BF16, "EFG"[a])[:])
+            w1_q[0, a] = quantise(grouped, "w1q0%d" % a, PACK if last else 1)
+            for t in range(PACK if a == 0 else 2):
+                for u in range(2):
+                    first_pass(banks0[t][u], 0, t, a, u)
+        for t in range(2, PACK):
+            for u in range(2):
+                for a in range(1, PASSES1):
+                    first_pass(banks0[t][u], 0, t, a, u)
+
+        for a, tag in enumerate(["words1", "rows1", "words2"]):
+            w1_raw[1, a] = [load_w(w1, a * K_PASS, K_PASS, K_PASS, tag)]
+
+        left = [held([P, PACK, PAIRS], F32, "left%d" % b) for b in range(PASSES2)]
+        right = [held([P, PACK, PAIRS], F32, "right%d" % b) for b in range(PASSES2)]
+        for t in range(PACK):
+            h = reading(banks0[t], 0, t, nc.vector if t == 0 else nc.scalar, "ABCD"[t])
+            pick(h, left[0], right[0], t)
+
+        banks1 = [[psum.tile([P, BANK], F32, name="bank") for u in range(2)] for t in range(PACK)]
+        wide = PACK * K_PASS
+        both = slot([P, 2 * wide], BF16, "D")
+        rounded = [slot([P, wide], BF16, "E")[:], both[:, 0:wide], both[:, wide : 2 * wide]]
+        for a in range(PASSES1):
+            grouped = round_w1(1, a, [nc.vector if a == 0 else nc.scalar], rounded[a])
+            w1_q[1, a] = quantise(grouped, "w1q1%d" % a, 1)
+            for t in range(PACK):
+                for u in range(2):
+                    first_pass(banks1[t][u], 1, t, a, u)
+        w2_word = slot([P, PASSES2, 2 * N], U8, "half0")
+        nc.sync.dma_start(w2_word[:].bitcast(I32), w2_words.rearrange("b p x -> p b x").bitcast(I32))
+        b3_sb = slot([P, N // P], F32, "words1")
+        with nc.allow_non_contiguous_dma(reason="one bias value to a partition"):
+            nc.sync.dma_start(b3_sb[:], b3.rearrange("(c p) -> p c", p=P))
+        w2_scale = slot([P, PASSES2 * N], U8, "half1")
+        nc.gpsimd.memset(w2_scale[:].bitcast(I32), 0)
+        for q in range(QUADS):
+            nc.sync.dma_start(
+                w2_scale[32 * q : 32 * q + 4, :].rearrange("r (b n) -> r b n", b=PASSES2).bitcast(I32),
+                w2_scales[:, 4 * q : 4 * q + 4, :].rearrange("b r n -> r b n").bitcast(I32),
+            )
+        w3_raw = [load_w(w3, b * K_PASS, 0, N, tag) for b, tag in enumerate(["rows1", "words2"])]
+        apart_bf0 = combine(left[0], right[0], ALU.subtract, "G")
+        joint_bf0 = combine(left[0], right[0], ALU.add, "D")
+        apart = [quantise(apart_bf0, "apart0", 1)]
+        joint = [quantise(joint_bf0, "joint0", 1)]
+        for t in range(PACK):
+            h = reading(banks1[t], 1, t, nc.scalar, "ABCA"[t])
+            pick(h, left[1], right[1], t)
+
+        w3_q = [quantise(round_w3(b, "FB"[b]), "w3q%d" % b, 1) for b in range(PASSES2)]
+
+        tiles = N // P
+        e_banks = [psum.tile([P, BANK], F32, name="bank") for c in range(tiles)]
+        f_banks = [psum.tile([P, BANK], F32, name="bank") for c in range(tiles)]
+
+        def e_pass(c, b):
+            codes, scales = apart[b]
+            nc.tensor.matmul_mx(
+                out=e_banks[c][:],
+                lhsT=w2_word[:, b, 2 * P * c : 2 * P * (c + 1)].bitcast(FP4X4),
+                lhsT_scale=w2_scale[:, b * N + P * c : b * N + P * (c + 1)],
+                rhs=codes[:].bitcast(FP8X4),
+                rhs_scale=scales[:],
+                start=(b == 0),
+                stop=(b == PASSES2 - 1),
+            )
+
+        def f_pass(c, b):
+            codes, scales = joint[b]
+            w_codes, w_scales = w3_q[b]
+            nc.tensor.matmul_mx(
+                out=f_banks[c][:],
+                lhsT=w_codes[:, P * c : P * (c + 1)].bitcast(FP8X4),
+                lhsT_scale=w_scales[:, P * c : P * (c + 1)],
+                rhs=codes[:].bitcast(FP8X4),
+                rhs_scale=scales[:],
+                start=(b == 0),
+                stop=(b == PASSES2 - 1),
+            )
+
+        for c in range(tiles):
+            e_pass(c, 0)
+        for c in range(tiles):
+            f_pass(c, 0)
+
+        apart_bf1 = combine(left[1], right[1], ALU.subtract, "G")
+        joint_bf1 = combine(left[1], right[1], ALU.add, "D")
+        apart.append(quantise(apart_bf1, "apart1", 1))
+        joint.append(quantise(joint_bf1, "joint1", 1))
+        size = []
+        for c in range(tiles):
+            e_pass(c, 1)
+            size.append(held([P, PAIRS], F32, "size%d" % c))
+            nc.scalar.activation(size[c][:], e_banks[c][:], ACT.Abs)
+        for c in range(tiles):
+            f_pass(c, 1)
+            result = held([P, PAIRS], F32, "result%d" % c)
+            nc.vector.scalar_tensor_tensor(
+                result[:], f_banks[c][:], b3_sb[:, c : c + 1], size[c][:], ALU.add, ALU.max
+            )
+            nc.sync.dma_start(out[P * c : P * (c + 1), :], result[:])

@@ -34,6 +34,7 @@ def tile_list_bone_pair_separation_kernel(
     with ExitStack() as ctx:
         keep = ctx.enter_context(tc.tile_pool(name="keep", bufs=1))
         ring = ctx.enter_context(tc.tile_pool(name="ring", bufs=2))
+        shared = ctx.enter_context(tc.tile_pool(name="shared", bufs=1))
         psum = ctx.enter_context(tc.psum_pool(name="psum", bufs=8))
 
         def held(shape, dtype, name):
@@ -46,7 +47,10 @@ def tile_list_bone_pair_separation_kernel(
         pos1_sb = keep.tile([P, PAIRS // 16], U16, name="pos1_sb")
         pos2_sb = keep.tile([P, PAIRS // 16], U16, name="pos2_sb")
 
-        tab_scale = held([P, T], U8, "tab_scale")
+        def placed(shape, dtype, name, offset):
+            return shared.tile(shape, dtype, name=name, align_bytes=64, offset=offset)
+
+        tab_scale = placed([P, T], U8, "tab_scale", 7 * 1024)
         for q in range(QUADS):
             (nc.vector if q % 2 else nc.gpsimd).memset(tab_scale[32 * q : 32 * q + FIRST_ROW, :].bitcast(I32), 0)
         picked_scale = held([P, S], U8, "picked_scale")
@@ -57,15 +61,16 @@ def tile_list_bone_pair_separation_kernel(
         def slot(shape, dtype, tag):
             return keep.tile(shape, dtype, name=tag, align_bytes=64)
 
-        def load_w(w, row0, col0, width, tag):
-            raw = slot([P, PACK, width], F32, tag)
+        def load_w(raw, w, row0, col0, width):
             nc.sync.dma_start(
-                raw[:], w[row0 : row0 + K_PASS, col0 : col0 + width].rearrange("(p j) c -> p j c", j=PACK)
+                raw, w[row0 : row0 + K_PASS, col0 : col0 + width].rearrange("(p j) c -> p j c", j=PACK)
             )
             return raw
 
-        def load_words(a):
-            words = slot([P, T], U16, "words%d" % a)
+        def load_rows(w, row0, col0, tag):
+            return load_w(slot([P, PACK, K_PASS], F32, tag)[:], w, row0, col0, K_PASS)
+
+        def load_words(words, a):
             nc.sync.dma_start(words[:].bitcast(I32), tab_words[a].bitcast(I32))
             return words
 
@@ -80,31 +85,38 @@ def tile_list_bone_pair_separation_kernel(
 
         nc.sync.dma_start(offs_sb[:], offs)
         load_scale_rows([0, 2])
-        tab_word = [load_words(0)]
+        tab_word = [load_words(slot([P, T], U16, "words0"), 0)]
         load_scale_rows([1, 3])
         w1_raw = {}
         half = K_PASS // 2
-        for a in range(PASSES1 - 1):
-            w1_raw[0, a] = [load_w(w1, a * K_PASS, 0, K_PASS, "rows%d" % a)]
-            tab_word.append(load_words(a + 1))
-        w1_raw[0, 2] = [load_w(w1, 2 * K_PASS, u * half, half, "half%d" % u) for u in range(2)]
+        w1_raw[0, 0] = [load_rows(w1, 0, 0, "rows0")]
+        tab_word.append(load_words(slot([P, T], U16, "words1"), 1))
+        w1_raw[0, 1] = [load_rows(w1, K_PASS, 0, "rows1")]
         nc.sync.dma_start(pos1_sb[:], pos1)
         nc.sync.dma_start(pos2_sb[:], pos2)
         gain_sb = held([P, PASSES2, PACK], F32, "gain_sb")
         nc.gpsimd.dma_start(gain_sb[:], gain.rearrange("(b p t) -> p b t", p=P, t=PACK))
 
-        v_word = [held([P, S], U16, "v_word%d" % a) for a in range(PASSES1)]
+        nc.vector.tensor_copy(picked_scale[:], tab_scale[:].indirect(offs_sb[:]))
+
+        def move_scales(a):
+            row = FIRST_ROW + 4 * a
+            nc.sync.dma_start(
+                v_scale[a][0:MOVED, :].bitcast(I32), picked_scale[row : row + MOVED, :].bitcast(I32)
+            )
+
+        move_scales(0)
+        tab_word.append(load_words(placed([P, T], U16, "words2", 0), 2))
+        move_scales(1)
+        halves = placed([P, 2, PACK, half], F32, "halves", 10 * 1024)
+        w1_raw[0, 2] = [load_w(halves[:, u], w1, 2 * K_PASS, u * half, half) for u in range(2)]
+        move_scales(2)
+
+        v_word = [placed([P, S], U16, "v_word0", 8 * 1024)]
+        v_word = v_word + [held([P, S], U16, "v_word%d" % a) for a in range(1, PASSES1)]
 
         def gather_words(a):
             nc.vector.tensor_copy(v_word[a][:], tab_word[a][:].indirect(offs_sb[:]))
-
-        def gather_scales():
-            nc.vector.tensor_copy(picked_scale[:], tab_scale[:].indirect(offs_sb[:]))
-            for a in range(PASSES1):
-                row = FIRST_ROW + 4 * a
-                nc.gpsimd.dma_start(
-                    v_scale[a][0:MOVED, :].bitcast(I32), picked_scale[row : row + MOVED, :].bitcast(I32)
-                )
 
         def copy_on(engine, dst, src):
             if engine is nc.scalar:
@@ -130,13 +142,13 @@ def tile_list_bone_pair_separation_kernel(
             parts = w1_raw[b, a]
             m = P // len(parts)
             for u, raw in enumerate(parts):
-                copy_on(engines[u], view[:, u * m : (u + 1) * m], raw[:].rearrange("p j (m t) -> p m j t", t=PACK))
+                copy_on(engines[u], view[:, u * m : (u + 1) * m], raw.rearrange("p j (m t) -> p m j t", t=PACK))
             return grouped
 
         def round_w3(b, tag):
             grouped = slot([P, PACK * N], BF16, tag)[:]
             dst = grouped.rearrange("p (c i j) -> p c j i", i=4, j=PACK)
-            src = w3_raw[b][:].rearrange("p j (c i) -> p c j i", i=4)
+            src = w3_raw[b].rearrange("p j (c i) -> p c j i", i=4)
             for u in range(2):
                 nc.scalar.copy(dst[:, 64 * u : 64 * (u + 1)], src[:, 64 * u : 64 * (u + 1)])
             return grouped
@@ -173,23 +185,22 @@ def tile_list_bone_pair_separation_kernel(
             nc.vector.tensor_copy(left[:, t, :], h[:].indirect(pos1_sb[:]))
             nc.vector.tensor_copy(right[:, t, :], h[:].indirect(pos2_sb[:]))
 
-        def combine(left, right, op, tag):
+        def combine(left, right, op, tag, pieces):
             grouped = slot([P, PACK * PAIRS], BF16, tag)[:]
-            nc.vector.tensor_tensor(
-                grouped.rearrange("p (c i t) -> p c t i", i=4, t=PACK),
-                left[:].rearrange("p t (c i) -> p c t i", i=4),
-                right[:].rearrange("p t (c i) -> p c t i", i=4),
-                op,
-            )
+            c = PAIRS // 4 // pieces
+            for u in range(pieces):
+                nc.vector.tensor_tensor(
+                    grouped.rearrange("p (c i t) -> p c t i", i=4, t=PACK)[:, u * c : (u + 1) * c],
+                    left[:].rearrange("p t (c i) -> p c t i", i=4)[:, u * c : (u + 1) * c],
+                    right[:].rearrange("p t (c i) -> p c t i", i=4)[:, u * c : (u + 1) * c],
+                    op,
+                )
             return grouped
 
-        gather_words(0)
-        gather_scales()
         banks0 = [[psum.tile([P, BANK], F32, name="bank") for u in range(2)] for t in range(PACK)]
         for a in range(PASSES1):
             last = a == PASSES1 - 1
-            if a > 0:
-                gather_words(a)
+            gather_words(a)
             grouped = round_w1(0, a, [nc.scalar, nc.vector], slot([P, PACK * K_PASS], BF16, "EFG"[a])[:])
             w1_q[0, a] = quantise(grouped, "w1q0%d" % a, PACK if last else 1)
             for t in range(PACK if a == 0 else 2):
@@ -200,8 +211,10 @@ def tile_list_bone_pair_separation_kernel(
                 for a in range(1, PASSES1):
                     first_pass(banks0[t][u], 0, t, a, u)
 
-        for a, tag in enumerate(["words1", "rows1", "words2"]):
-            w1_raw[1, a] = [load_w(w1, a * K_PASS, K_PASS, K_PASS, tag)]
+        halves1 = slot([P, 2, PACK, half], F32, "words1")
+        w1_raw[1, 0] = [load_w(halves1[:, u], w1, 0, K_PASS + u * half, half) for u in range(2)]
+        w1_raw[1, 1] = [load_rows(w1, K_PASS, K_PASS, "rows1")]
+        w1_raw[1, 2] = [load_w(placed([P, PACK, K_PASS], F32, "rows12", 0)[:], w1, 2 * K_PASS, K_PASS, K_PASS)]
 
         left = [held([P, PACK, PAIRS], F32, "left%d" % b) for b in range(PASSES2)]
         right = [held([P, PACK, PAIRS], F32, "right%d" % b) for b in range(PASSES2)]
@@ -214,26 +227,31 @@ def tile_list_bone_pair_separation_kernel(
         both = slot([P, 2 * wide], BF16, "D")
         rounded = [slot([P, wide], BF16, "E")[:], both[:, 0:wide], both[:, wide : 2 * wide]]
         for a in range(PASSES1):
-            grouped = round_w1(1, a, [nc.vector if a == 0 else nc.scalar], rounded[a])
+            grouped = round_w1(1, a, [nc.vector, nc.vector] if a == 0 else [nc.scalar], rounded[a])
             w1_q[1, a] = quantise(grouped, "w1q1%d" % a, 1)
-            for t in range(PACK):
+            for t in range(PACK if a == 0 else 1):
                 for u in range(2):
                     first_pass(banks1[t][u], 1, t, a, u)
-        w2_word = slot([P, PASSES2, 2 * N], U8, "half0")
+        for t in range(1, PACK):
+            for u in range(2):
+                for a in range(1, PASSES1):
+                    first_pass(banks1[t][u], 1, t, a, u)
+        w2_word = placed([P, PASSES2, 2 * N], U8, "w2_word", 10 * 1024)
         nc.sync.dma_start(w2_word[:].bitcast(I32), w2_words.rearrange("b p x -> p b x").bitcast(I32))
         b3_sb = slot([P, N // P], F32, "words1")
         with nc.allow_non_contiguous_dma(reason="one bias value to a partition"):
             nc.sync.dma_start(b3_sb[:], b3.rearrange("(c p) -> p c", p=P))
-        w2_scale = slot([P, PASSES2 * N], U8, "half1")
+        w2_scale = placed([P, PASSES2 * N], U8, "w2_scale", 14 * 1024)
         nc.gpsimd.memset(w2_scale[:].bitcast(I32), 0)
         for q in range(QUADS):
             nc.sync.dma_start(
                 w2_scale[32 * q : 32 * q + 4, :].rearrange("r (b n) -> r b n", b=PASSES2).bitcast(I32),
                 w2_scales[:, 4 * q : 4 * q + 4, :].rearrange("b r n -> r b n").bitcast(I32),
             )
-        w3_raw = [load_w(w3, b * K_PASS, 0, N, tag) for b, tag in enumerate(["rows1", "words2"])]
-        apart_bf0 = combine(left[0], right[0], ALU.subtract, "G")
-        joint_bf0 = combine(left[0], right[0], ALU.add, "D")
+        w3_raw = [load_rows(w3, 0, 0, "rows1")]
+        w3_raw.append(load_w(placed([P, PACK, N], F32, "rows31", 0)[:], w3, K_PASS, 0, N))
+        apart_bf0 = combine(left[0], right[0], ALU.subtract, "G", 1)
+        joint_bf0 = combine(left[0], right[0], ALU.add, "D", 1)
         apart = [quantise(apart_bf0, "apart0", 1)]
         joint = [quantise(joint_bf0, "joint0", 1)]
         for t in range(PACK):
@@ -276,10 +294,8 @@ def tile_list_bone_pair_separation_kernel(
         for c in range(tiles):
             f_pass(c, 0)
 
-        apart_bf1 = combine(left[1], right[1], ALU.subtract, "G")
-        joint_bf1 = combine(left[1], right[1], ALU.add, "D")
-        apart.append(quantise(apart_bf1, "apart1", 1))
-        joint.append(quantise(joint_bf1, "joint1", 1))
+        apart.append(quantise(combine(left[1], right[1], ALU.subtract, "G", 2), "apart1", 2))
+        joint.append(quantise(combine(left[1], right[1], ALU.add, "D", 2), "joint1", 2))
         size = []
         for c in range(tiles):
             e_pass(c, 1)

@@ -145,8 +145,7 @@ def tile_list_bone_pair_separation_kernel(
                 copy_on(engines[u], view[:, u * m : (u + 1) * m], raw.rearrange("p j (m t) -> p m j t", t=PACK))
             return grouped
 
-        def round_w3(b, tag):
-            grouped = slot([P, PACK * N], BF16, tag)[:]
+        def round_w3(b, grouped):
             dst = grouped.rearrange("p (c i j) -> p c j i", i=4, j=PACK)
             src = w3_raw[b].rearrange("p j (c i) -> p c j i", i=4)
             for u in range(2):
@@ -175,15 +174,17 @@ def tile_list_bone_pair_separation_kernel(
             g = gain_sb[:, b, t : t + 1]
             if gain_engine is nc.scalar:
                 nc.scalar.activation(h[:], tanh[:], ACT.Copy, scale=g)
+            elif gain_engine is nc.gpsimd:
+                nc.gpsimd.tensor_scalar(h[:], tanh[:], g, 0.0, ALU.mult, ALU.add)
             else:
                 for u in range(2):
                     cols = slice(u * BANK, (u + 1) * BANK)
                     nc.vector.tensor_scalar(h[:, cols], tanh[:, cols], g, None, ALU.mult)
             return h
 
-        def pick(h, left, right, t):
-            nc.vector.tensor_copy(left[:, t, :], h[:].indirect(pos1_sb[:]))
-            nc.vector.tensor_copy(right[:, t, :], h[:].indirect(pos2_sb[:]))
+        def pick(h, left, right):
+            nc.vector.tensor_copy(left, h[:].indirect(pos1_sb[:]))
+            nc.vector.tensor_copy(right, h[:].indirect(pos2_sb[:]))
 
         def combine(left, right, op, tag, pieces):
             grouped = slot([P, PACK * PAIRS], BF16, tag)[:]
@@ -216,16 +217,14 @@ def tile_list_bone_pair_separation_kernel(
         w1_raw[1, 1] = [load_rows(w1, K_PASS, K_PASS, "rows1")]
         w1_raw[1, 2] = [load_w(placed([P, PACK, K_PASS], F32, "rows12", 0)[:], w1, 2 * K_PASS, K_PASS, K_PASS)]
 
-        left = [held([P, PACK, PAIRS], F32, "left%d" % b) for b in range(PASSES2)]
-        right = [held([P, PACK, PAIRS], F32, "right%d" % b) for b in range(PASSES2)]
-        for t in range(PACK):
-            h = reading(banks0[t], 0, t, nc.vector if t == 0 else nc.scalar, "ABCD"[t])
-            pick(h, left[0], right[0], t)
+        h0 = [reading(banks0[t], 0, t, nc.vector if t == 0 else nc.gpsimd, "ABCD"[t]) for t in range(PACK)]
+        pairs0 = [held([P, 2, PAIRS], F32, "pairs0%d" % t) for t in range(PACK - 1)]
+        for t in range(PACK - 1):
+            pick(h0[t], pairs0[t][:, 0], pairs0[t][:, 1])
 
         banks1 = [[psum.tile([P, BANK], F32, name="bank") for u in range(2)] for t in range(PACK)]
         wide = PACK * K_PASS
-        both = slot([P, 2 * wide], BF16, "D")
-        rounded = [slot([P, wide], BF16, "E")[:], both[:, 0:wide], both[:, wide : 2 * wide]]
+        rounded = [slot([P, wide], BF16, tag)[:] for tag in "EAB"]
         for a in range(PASSES1):
             grouped = round_w1(1, a, [nc.vector, nc.vector] if a == 0 else [nc.scalar], rounded[a])
             w1_q[1, a] = quantise(grouped, "w1q1%d" % a, 1)
@@ -236,29 +235,49 @@ def tile_list_bone_pair_separation_kernel(
             for u in range(2):
                 for a in range(1, PASSES1):
                     first_pass(banks1[t][u], 1, t, a, u)
-        w2_word = placed([P, PASSES2, 2 * N], U8, "w2_word", 10 * 1024)
+        pairs0.append(slot([P, 2, PAIRS], F32, "B"))
+        pick(h0[PACK - 1], pairs0[PACK - 1][:, 0], pairs0[PACK - 1][:, 1])
+        planes = slot([P, 2, PACK, PAIRS], BF16, "D")
+        for t in range(PACK):
+            for x, op in enumerate([ALU.subtract, ALU.add]):
+                nc.gpsimd.tensor_tensor(planes[:, x, t], pairs0[t][:, 0], pairs0[t][:, 1], op)
+        w2_word = slot([P, PASSES2, 2 * N], U8, "F")
         nc.sync.dma_start(w2_word[:].bitcast(I32), w2_words.rearrange("b p x -> p b x").bitcast(I32))
         b3_sb = slot([P, N // P], F32, "words1")
         with nc.allow_non_contiguous_dma(reason="one bias value to a partition"):
             nc.sync.dma_start(b3_sb[:], b3.rearrange("(c p) -> p c", p=P))
-        w2_scale = placed([P, PASSES2 * N], U8, "w2_scale", 14 * 1024)
+        w2_scale = slot([P, PASSES2 * N], U8, "G")
         nc.gpsimd.memset(w2_scale[:].bitcast(I32), 0)
         for q in range(QUADS):
             nc.sync.dma_start(
                 w2_scale[32 * q : 32 * q + 4, :].rearrange("r (b n) -> r b n", b=PASSES2).bitcast(I32),
                 w2_scales[:, 4 * q : 4 * q + 4, :].rearrange("b r n -> r b n").bitcast(I32),
             )
-        w3_raw = [load_rows(w3, 0, 0, "rows1")]
+        w3_raw = [load_w(placed([P, PACK, N], F32, "rows30", 10 * 1024)[:], w3, 0, 0, N)]
         w3_raw.append(load_w(placed([P, PACK, N], F32, "rows31", 0)[:], w3, K_PASS, 0, N))
-        apart_bf0 = combine(left[0], right[0], ALU.subtract, "G", 1)
-        joint_bf0 = combine(left[0], right[0], ALU.add, "D", 1)
-        apart = [quantise(apart_bf0, "apart0", 1)]
-        joint = [quantise(joint_bf0, "joint0", 1)]
+        left = held([P, PACK, PAIRS], F32, "left")
+        right = held([P, PACK, PAIRS], F32, "right")
         for t in range(PACK):
-            h = reading(banks1[t], 1, t, nc.scalar, "ABCA"[t])
-            pick(h, left[1], right[1], t)
+            h = reading(banks1[t], 1, t, nc.vector if t == 0 else nc.scalar, ["A", "rows1", "C", "H"][t])
+            pick(h, left[:, t], right[:, t])
 
-        w3_q = [quantise(round_w3(b, "FB"[b]), "w3q%d" % b, 1) for b in range(PASSES2)]
+        w3_bf0 = round_w3(0, slot([P, wide], BF16, "words0")[:])
+        late = slot([P, 3 * wide], BF16, "H")
+
+        def weave(x):
+            grouped = late[:, x * wide : (x + 1) * wide]
+            nc.scalar.copy(
+                grouped.rearrange("p (c i t) -> p c t i", i=4, t=PACK),
+                planes[:, x].rearrange("p t (c i) -> p c t i", i=4),
+            )
+            return grouped
+
+        apart = {1: quantise(combine(left, right, ALU.subtract, "E", 2), "apart1", 2)}
+        joint = {1: quantise(combine(left, right, ALU.add, "rows0", 2), "joint1", 2)}
+        w3_bf1 = round_w3(1, late[:, 2 * wide : 3 * wide])
+        w3_q = [quantise(w3_bf0, "w3q0", 1), quantise(w3_bf1, "w3q1", 1)]
+        apart[0] = quantise(weave(0), "apart0", 1)
+        joint[0] = quantise(weave(1), "joint0", 1)
 
         tiles = N // P
         e_banks = [psum.tile([P, BANK], F32, name="bank") for c in range(tiles)]
@@ -272,8 +291,8 @@ def tile_list_bone_pair_separation_kernel(
                 lhsT_scale=w2_scale[:, b * N + P * c : b * N + P * (c + 1)],
                 rhs=codes[:].bitcast(FP8X4),
                 rhs_scale=scales[:],
-                start=(b == 0),
-                stop=(b == PASSES2 - 1),
+                start=(b == 1),
+                stop=(b == 0),
             )
 
         def f_pass(c, b):
@@ -285,24 +304,21 @@ def tile_list_bone_pair_separation_kernel(
                 lhsT_scale=w_scales[:, P * c : P * (c + 1)],
                 rhs=codes[:].bitcast(FP8X4),
                 rhs_scale=scales[:],
-                start=(b == 0),
-                stop=(b == PASSES2 - 1),
+                start=(b == 1),
+                stop=(b == 0),
             )
 
         for c in range(tiles):
-            e_pass(c, 0)
+            e_pass(c, 1)
         for c in range(tiles):
-            f_pass(c, 0)
-
-        apart.append(quantise(combine(left[1], right[1], ALU.subtract, "G", 2), "apart1", 2))
-        joint.append(quantise(combine(left[1], right[1], ALU.add, "D", 2), "joint1", 2))
+            f_pass(c, 1)
         size = []
         for c in range(tiles):
-            e_pass(c, 1)
+            e_pass(c, 0)
             size.append(held([P, PAIRS], F32, "size%d" % c))
             nc.scalar.activation(size[c][:], e_banks[c][:], ACT.Abs)
         for c in range(tiles):
-            f_pass(c, 1)
+            f_pass(c, 0)
             result = held([P, PAIRS], F32, "result%d" % c)
             nc.vector.scalar_tensor_tensor(
                 result[:], f_banks[c][:], b3_sb[:, c : c + 1], size[c][:], ALU.add, ALU.max

@@ -20,11 +20,22 @@ P = 128
 PACK = 4
 K_PASS = P * PACK
 BANK = 512
+BANKS = 8
+WIDE = PACK * K_PASS
+HALF = K_PASS // 2
 PASSES1 = K // K_PASS
 PASSES2 = H // K_PASS
 QUADS = 4
-FIRST_ROW = 32 - 4 * PASSES1
-MOVED = 100
+QUAD = P // QUADS
+QUAD_ROWS = 4
+LINE = 4
+LIST_ROWS = 16
+FIRST_ROW = QUAD - QUAD_ROWS * PASSES1
+MOVED = (QUADS - 1) * QUAD + QUAD_ROWS
+
+KB = 1024
+WORDS2_AT, TAB_SCALE_AT, V_WORD0_AT, HALVES_AT = 0, 7 * KB, 8 * KB, 10 * KB
+APART_AT, LAST_TANH_AT, LATE_AT = 18 * KB, 20 * KB, 22 * KB
 
 
 def tile_list_bone_pair_separation_kernel(
@@ -33,33 +44,31 @@ def tile_list_bone_pair_separation_kernel(
     nc = tc.nc
     with ExitStack() as ctx:
         keep = ctx.enter_context(tc.tile_pool(name="keep", bufs=1))
-        ring = ctx.enter_context(tc.tile_pool(name="ring", bufs=2))
+        ring = ctx.enter_context(tc.tile_pool(name="ring", bufs=PACK))
         shared = ctx.enter_context(tc.tile_pool(name="shared", bufs=1))
-        psum = ctx.enter_context(tc.psum_pool(name="psum", bufs=8))
+        psum = ctx.enter_context(tc.psum_pool(name="psum", bufs=BANKS))
 
         def held(shape, dtype, name):
             return keep.tile(shape, dtype, name=name, align_bytes=64)
 
-        def turned(shape, dtype, name, bufs):
-            return ring.tile(shape, dtype, name=name, align_bytes=64, bufs=bufs)
-
-        offs_sb = keep.tile([P, S // 16], U16, name="offs_sb")
-        pos1_sb = keep.tile([P, PAIRS // 16], U16, name="pos1_sb")
-        pos2_sb = keep.tile([P, PAIRS // 16], U16, name="pos2_sb")
-
         def placed(shape, dtype, name, offset):
             return shared.tile(shape, dtype, name=name, align_bytes=64, offset=offset)
 
-        tab_scale = placed([P, T], U8, "tab_scale", 7 * 1024)
+        def new_banks(count):
+            return [psum.tile([P, BANK], F32, name="bank") for i in range(count)]
+
+        offs_sb = keep.tile([P, S // LIST_ROWS], U16, name="offs_sb")
+        pos1_sb = keep.tile([P, PAIRS // LIST_ROWS], U16, name="pos1_sb")
+        pos2_sb = keep.tile([P, PAIRS // LIST_ROWS], U16, name="pos2_sb")
+
+        tab_scale = placed([P, T], U8, "tab_scale", TAB_SCALE_AT)
         for q in range(QUADS):
-            (nc.vector if q % 2 else nc.gpsimd).memset(tab_scale[32 * q : 32 * q + FIRST_ROW, :].bitcast(I32), 0)
+            engine = nc.vector if q % 2 else nc.gpsimd
+            engine.memset(tab_scale[QUAD * q : QUAD * q + FIRST_ROW, :].bitcast(I32), 0)
         picked_scale = held([P, S], U8, "picked_scale")
         v_scale = [held([P, S], U8, "v_scale%d" % a) for a in range(PASSES1)]
         for a in range(PASSES1):
             nc.vector.memset(v_scale[a][:].bitcast(I32), 0)
-
-        def slot(shape, dtype, tag):
-            return keep.tile(shape, dtype, name=tag, align_bytes=64)
 
         def load_w(raw, w, row0, col0, width):
             nc.sync.dma_start(
@@ -67,31 +76,29 @@ def tile_list_bone_pair_separation_kernel(
             )
             return raw
 
-        def load_rows(w, row0, col0, tag):
-            return load_w(slot([P, PACK, K_PASS], F32, tag)[:], w, row0, col0, K_PASS)
+        def load_chunk(tile, w, row0, col0):
+            return [load_w(tile[:], w, row0, col0, K_PASS)]
+
+        def load_halves(tile, w, row0, col0):
+            return [load_w(tile[:, u], w, row0, col0 + u * HALF, HALF) for u in range(2)]
 
         def load_words(words, a):
             nc.sync.dma_start(words[:].bitcast(I32), tab_words[a].bitcast(I32))
             return words
 
-        def load_scale_rows(quads):
-            for a in range(PASSES1):
-                for q in quads:
-                    row = 32 * q + FIRST_ROW + 4 * a
-                    nc.sync.dma_start(
-                        tab_scale[row : row + 4, :].bitcast(I32),
-                        tab_scales[a, 4 * q : 4 * q + 4, :].bitcast(I32),
-                    )
+        chunk_shape, halves_shape = [P, PACK, K_PASS], [P, 2, PACK, HALF]
 
         nc.sync.dma_start(offs_sb[:], offs)
-        load_scale_rows([0, 2])
-        tab_word = [load_words(slot([P, T], U16, "words0"), 0)]
-        load_scale_rows([1, 3])
+        tab_word = [load_words(held([P, T], U16, "words0"), 0)]
+        for q in range(QUADS):
+            nc.sync.dma_start(
+                tab_scale[QUAD * q + FIRST_ROW : QUAD * (q + 1), :].bitcast(I32),
+                tab_scales[:, QUAD_ROWS * q : QUAD_ROWS * (q + 1), :].bitcast(I32),
+            )
         w1_raw = {}
-        half = K_PASS // 2
-        w1_raw[0, 0] = [load_rows(w1, 0, 0, "rows0")]
-        tab_word.append(load_words(slot([P, T], U16, "words1"), 1))
-        w1_raw[0, 1] = [load_rows(w1, K_PASS, 0, "rows1")]
+        w1_raw[0, 0] = load_chunk(held(chunk_shape, F32, "rows0"), w1, 0, 0)
+        tab_word.append(load_words(held([P, T], U16, "words1"), 1))
+        w1_raw[0, 1] = load_chunk(held(chunk_shape, F32, "rows1"), w1, K_PASS, 0)
         nc.sync.dma_start(pos1_sb[:], pos1)
         nc.sync.dma_start(pos2_sb[:], pos2)
         gain_sb = held([P, PASSES2, PACK], F32, "gain_sb")
@@ -100,64 +107,57 @@ def tile_list_bone_pair_separation_kernel(
         nc.vector.tensor_copy(picked_scale[:], tab_scale[:].indirect(offs_sb[:]))
 
         def move_scales(a):
-            row = FIRST_ROW + 4 * a
+            row = FIRST_ROW + QUAD_ROWS * a
             nc.sync.dma_start(
                 v_scale[a][0:MOVED, :].bitcast(I32), picked_scale[row : row + MOVED, :].bitcast(I32)
             )
 
         move_scales(0)
-        tab_word.append(load_words(placed([P, T], U16, "words2", 0), 2))
+        tab_word.append(load_words(placed([P, T], U16, "words2", WORDS2_AT), 2))
         move_scales(1)
-        halves = placed([P, 2, PACK, half], F32, "halves", 10 * 1024)
-        w1_raw[0, 2] = [load_w(halves[:, u], w1, 2 * K_PASS, u * half, half) for u in range(2)]
+        w1_raw[0, 2] = load_halves(placed(halves_shape, F32, "halves", HALVES_AT), w1, 2 * K_PASS, 0)
         move_scales(2)
 
-        v_word = [placed([P, S], U16, "v_word0", 8 * 1024)]
-        v_word = v_word + [held([P, S], U16, "v_word%d" % a) for a in range(1, PASSES1)]
+        v_word = [placed([P, S], U16, "v_word0", V_WORD0_AT)]
+        v_word.extend(held([P, S], U16, "v_word%d" % a) for a in range(1, PASSES1))
 
-        def gather_words(a):
-            nc.vector.tensor_copy(v_word[a][:], tab_word[a][:].indirect(offs_sb[:]))
-
-        def copy_on(engine, dst, src):
-            if engine is nc.scalar:
-                nc.scalar.copy(dst, src)
-            else:
-                engine.tensor_copy(dst, src)
-
-        def quantise(grouped, name, pieces):
-            words = K_PASS
-            codes = held([P, words], U32, name + "_codes")
-            scales = held([P, words], U8, name + "_scales")
-            w = words // pieces
+        def quantise(rounded, name, pieces):
+            codes = held([P, K_PASS], U32, name + "_codes")
+            scales = held([P, K_PASS], U8, name + "_scales")
+            w = K_PASS // pieces
             for i in range(pieces):
                 nc.vector.quantize_mx(
                     out=codes[:, i * w : (i + 1) * w].bitcast(FP8X4),
                     scales=scales[:, i * w : (i + 1) * w],
-                    in_=grouped[:, PACK * i * w : PACK * (i + 1) * w],
+                    in_=rounded[:, PACK * i * w : PACK * (i + 1) * w],
                 )
             return codes, scales
 
-        def round_w1(b, a, engines, grouped):
-            view = grouped.rearrange("p (t m j) -> p m j t", t=PACK, j=PACK)
-            parts = w1_raw[b, a]
-            m = P // len(parts)
-            for u, raw in enumerate(parts):
-                copy_on(engines[u], view[:, u * m : (u + 1) * m], raw.rearrange("p j (m t) -> p m j t", t=PACK))
-            return grouped
+        def round_w1(b, a, copies, rounded):
+            dst = rounded.rearrange("p (t m j) -> p m j t", t=PACK, j=PACK)
+            m = P // len(copies)
+            for u, copy in enumerate(copies):
+                copy(dst[:, u * m : (u + 1) * m], w1_raw[b, a][u].rearrange("p j (m t) -> p m j t", t=PACK))
+            return rounded
 
-        def round_w3(b, grouped):
-            dst = grouped.rearrange("p (c i j) -> p c j i", i=4, j=PACK)
-            src = w3_raw[b].rearrange("p j (c i) -> p c j i", i=4)
-            for u in range(2):
-                nc.scalar.copy(dst[:, 64 * u : 64 * (u + 1)], src[:, 64 * u : 64 * (u + 1)])
-            return grouped
+        def woven(rounded):
+            return rounded.rearrange("p (c i t) -> p c t i", i=LINE, t=PACK)
+
+        def planar(planes):
+            return planes.rearrange("p t (c i) -> p c t i", i=LINE)
+
+        def weave(rounded, planes, pieces):
+            c = K_PASS // LINE // pieces
+            for u in range(pieces):
+                nc.scalar.copy(woven(rounded)[:, u * c : (u + 1) * c], planar(planes)[:, u * c : (u + 1) * c])
+            return rounded
 
         w1_q = {}
 
-        def first_pass(bank, b, t, a, u):
+        def first_pass(banks, b, t, a, u):
             codes, scales = w1_q[b, a]
             nc.tensor.matmul_mx(
-                out=bank[:],
+                out=banks[t][u][:],
                 lhsT=codes[:, t * P : (t + 1) * P].bitcast(FP8X4),
                 lhsT_scale=scales[:, t * P : (t + 1) * P],
                 rhs=v_word[a][:, u * BANK : (u + 1) * BANK].bitcast(FP4X4),
@@ -166,159 +166,156 @@ def tile_list_bone_pair_separation_kernel(
                 stop=(a == PASSES1 - 1),
             )
 
-        def reading(banks, b, t, gain_engine, tag):
-            tanh = slot([P, S], F32, tag)
-            for u in range(2):
-                nc.scalar.activation(tanh[:, u * BANK : (u + 1) * BANK], banks[u][:], ACT.Tanh)
-            h = turned([P, S], F32, "h", 4)
-            g = gain_sb[:, b, t : t + 1]
-            if gain_engine is nc.scalar:
-                nc.scalar.activation(h[:], tanh[:], ACT.Copy, scale=g)
-            elif gain_engine is nc.gpsimd:
-                nc.gpsimd.tensor_scalar(h[:], tanh[:], g, 0.0, ALU.mult, ALU.add)
-            else:
-                for u in range(2):
-                    cols = slice(u * BANK, (u + 1) * BANK)
-                    nc.vector.tensor_scalar(h[:, cols], tanh[:, cols], g, None, ALU.mult)
+        def first_stage(b, quantised_w1, ahead):
+            banks = [new_banks(S // BANK) for t in range(PACK)]
+            for a in range(PASSES1):
+                w1_q[b, a] = quantised_w1(a)
+                for t in range(PACK if a == 0 else ahead):
+                    for u in range(S // BANK):
+                        first_pass(banks, b, t, a, u)
+            for t in range(ahead, PACK):
+                for u in range(S // BANK):
+                    for a in range(1, PASSES1):
+                        first_pass(banks, b, t, a, u)
+            return banks
+
+        def gain_on_vector(h, tanh, g):
+            for u in range(S // BANK):
+                cols = slice(u * BANK, (u + 1) * BANK)
+                nc.vector.tensor_scalar(h[:, cols], tanh[:, cols], g, None, ALU.mult)
+
+        def gain_on_gpsimd(h, tanh, g):
+            nc.gpsimd.tensor_scalar(h[:], tanh[:], g, 0.0, ALU.mult, ALU.add)
+
+        def gain_on_scalar(h, tanh, g):
+            nc.scalar.activation(h[:], tanh[:], ACT.Copy, scale=g)
+
+        def make_slice(banks, b, t, tanh, apply_gain):
+            for u in range(S // BANK):
+                nc.scalar.activation(tanh[:, u * BANK : (u + 1) * BANK], banks[t][u][:], ACT.Tanh)
+            h = ring.tile([P, S], F32, name="h", align_bytes=64)
+            apply_gain(h, tanh, gain_sb[:, b, t : t + 1])
             return h
 
         def pick(h, left, right):
             nc.vector.tensor_copy(left, h[:].indirect(pos1_sb[:]))
             nc.vector.tensor_copy(right, h[:].indirect(pos2_sb[:]))
 
-        def combine(left, right, op, tag, pieces):
-            grouped = slot([P, PACK * PAIRS], BF16, tag)[:]
-            c = PAIRS // 4 // pieces
-            for u in range(pieces):
-                nc.vector.tensor_tensor(
-                    grouped.rearrange("p (c i t) -> p c t i", i=4, t=PACK)[:, u * c : (u + 1) * c],
-                    left[:].rearrange("p t (c i) -> p c t i", i=4)[:, u * c : (u + 1) * c],
-                    right[:].rearrange("p t (c i) -> p c t i", i=4)[:, u * c : (u + 1) * c],
-                    op,
-                )
-            return grouped
-
-        banks0 = [[psum.tile([P, BANK], F32, name="bank") for u in range(2)] for t in range(PACK)]
-        for a in range(PASSES1):
+        def quantised_w1_low(a):
+            nc.vector.tensor_copy(v_word[a][:], tab_word[a][:].indirect(offs_sb[:]))
             last = a == PASSES1 - 1
-            gather_words(a)
-            grouped = round_w1(0, a, [nc.scalar, nc.vector], slot([P, PACK * K_PASS], BF16, "EFG"[a])[:])
-            w1_q[0, a] = quantise(grouped, "w1q0%d" % a, PACK if last else 1)
-            for t in range(PACK if a == 0 else 2):
-                for u in range(2):
-                    first_pass(banks0[t][u], 0, t, a, u)
-        for t in range(2, PACK):
-            for u in range(2):
-                for a in range(1, PASSES1):
-                    first_pass(banks0[t][u], 0, t, a, u)
+            copies = [nc.scalar.copy, nc.vector.tensor_copy] if last else [nc.scalar.copy]
+            rounded = round_w1(0, a, copies, held([P, WIDE], BF16, "round%d" % a)[:])
+            return quantise(rounded, "w1q0%d" % a, PACK if last else 1)
 
-        halves1 = slot([P, 2, PACK, half], F32, "words1")
-        w1_raw[1, 0] = [load_w(halves1[:, u], w1, 0, K_PASS + u * half, half) for u in range(2)]
-        w1_raw[1, 1] = [load_rows(w1, K_PASS, K_PASS, "rows1")]
-        w1_raw[1, 2] = [load_w(placed([P, PACK, K_PASS], F32, "rows12", 0)[:], w1, 2 * K_PASS, K_PASS, K_PASS)]
+        banks0 = first_stage(0, quantised_w1_low, 2)
 
-        h0 = [reading(banks0[t], 0, t, nc.vector if t == 0 else nc.gpsimd, "ABCD"[t]) for t in range(PACK)]
+        w1_raw[1, 0] = load_halves(held(halves_shape, F32, "words1"), w1, 0, K_PASS)
+        w1_raw[1, 1] = load_chunk(held(chunk_shape, F32, "rows1"), w1, K_PASS, K_PASS)
+        w1_raw[1, 2] = load_chunk(placed(chunk_shape, F32, "rows12", WORDS2_AT), w1, 2 * K_PASS, K_PASS)
+
+        h0 = [
+            make_slice(banks0, 0, t, held([P, S], F32, "tanh%d" % t), gain_on_gpsimd if t else gain_on_vector)
+            for t in range(PACK)
+        ]
         pairs0 = [held([P, 2, PAIRS], F32, "pairs0%d" % t) for t in range(PACK - 1)]
         for t in range(PACK - 1):
             pick(h0[t], pairs0[t][:, 0], pairs0[t][:, 1])
 
-        banks1 = [[psum.tile([P, BANK], F32, name="bank") for u in range(2)] for t in range(PACK)]
-        wide = PACK * K_PASS
-        rounded = [slot([P, wide], BF16, tag)[:] for tag in "EAB"]
-        for a in range(PASSES1):
-            grouped = round_w1(1, a, [nc.vector, nc.vector] if a == 0 else [nc.scalar], rounded[a])
-            w1_q[1, a] = quantise(grouped, "w1q1%d" % a, 1)
-            for t in range(PACK if a == 0 else 1):
-                for u in range(2):
-                    first_pass(banks1[t][u], 1, t, a, u)
-        for t in range(1, PACK):
-            for u in range(2):
-                for a in range(1, PASSES1):
-                    first_pass(banks1[t][u], 1, t, a, u)
-        pairs0.append(slot([P, 2, PAIRS], F32, "B"))
+        rounded1 = [held([P, WIDE], BF16, name)[:] for name in ["round0", "tanh0", "tanh1"]]
+
+        def quantised_w1_high(a):
+            copies = [nc.scalar.copy] if a else [nc.vector.tensor_copy, nc.vector.tensor_copy]
+            return quantise(round_w1(1, a, copies, rounded1[a]), "w1q1%d" % a, 1)
+
+        banks1 = first_stage(1, quantised_w1_high, 1)
+
+        pairs0.append(held([P, 2, PAIRS], F32, "tanh1"))
         pick(h0[PACK - 1], pairs0[PACK - 1][:, 0], pairs0[PACK - 1][:, 1])
-        planes = slot([P, 2, PACK, PAIRS], BF16, "D")
+        planes0 = held([P, 2, PACK, PAIRS], BF16, "tanh3")
         for t in range(PACK):
             for x, op in enumerate([ALU.subtract, ALU.add]):
-                nc.gpsimd.tensor_tensor(planes[:, x, t], pairs0[t][:, 0], pairs0[t][:, 1], op)
-        w2_word = slot([P, PASSES2, 2 * N], U8, "F")
+                nc.gpsimd.tensor_tensor(planes0[:, x, t], pairs0[t][:, 0], pairs0[t][:, 1], op)
+
+        w2_word = held([P, PASSES2, 2 * N], U8, "round1")
         nc.sync.dma_start(w2_word[:].bitcast(I32), w2_words.rearrange("b p x -> p b x").bitcast(I32))
-        b3_sb = slot([P, N // P], F32, "words1")
+        b3_sb = held([P, N // P], F32, "words1")
         with nc.allow_non_contiguous_dma(reason="one bias value to a partition"):
             nc.sync.dma_start(b3_sb[:], b3.rearrange("(c p) -> p c", p=P))
-        w2_scale = slot([P, PASSES2 * N], U8, "G")
+        w2_scale = held([P, PASSES2 * N], U8, "round2")
         nc.gpsimd.memset(w2_scale[:].bitcast(I32), 0)
         for q in range(QUADS):
             nc.sync.dma_start(
-                w2_scale[32 * q : 32 * q + 4, :].rearrange("r (b n) -> r b n", b=PASSES2).bitcast(I32),
-                w2_scales[:, 4 * q : 4 * q + 4, :].rearrange("b r n -> r b n").bitcast(I32),
+                w2_scale[QUAD * q : QUAD * q + QUAD_ROWS, :].rearrange("r (b n) -> r b n", b=PASSES2).bitcast(I32),
+                w2_scales[:, QUAD_ROWS * q : QUAD_ROWS * (q + 1), :].rearrange("b r n -> r b n").bitcast(I32),
             )
-        w3_raw = [load_w(placed([P, PACK, N], F32, "rows30", 10 * 1024)[:], w3, 0, 0, N)]
-        w3_raw.append(load_w(placed([P, PACK, N], F32, "rows31", 0)[:], w3, K_PASS, 0, N))
+        w3_raw = [
+            load_w(placed(chunk_shape, F32, "rows3%d" % b, at)[:], w3, b * K_PASS, 0, N)
+            for b, at in enumerate([HALVES_AT, WORDS2_AT])
+        ]
+
         left = held([P, PACK, PAIRS], F32, "left")
         right = held([P, PACK, PAIRS], F32, "right")
+        sums1 = held([P, PACK, PAIRS], BF16, "sums1")
+        tanh1 = [held([P, S], F32, name) for name in ["tanh0", "rows1", "tanh2"]]
+        tanh1.append(placed([P, S], F32, "tanh13", LAST_TANH_AT))
         for t in range(PACK):
-            h = reading(banks1[t], 1, t, nc.vector if t == 0 else nc.scalar, ["A", "rows1", "C", "H"][t])
+            h = make_slice(banks1, 1, t, tanh1[t], gain_on_scalar if t else gain_on_vector)
             pick(h, left[:, t], right[:, t])
+            engine = nc.gpsimd if t < PACK - 1 else nc.vector
+            engine.tensor_tensor(sums1[:, t], left[:, t], right[:, t], ALU.add)
 
-        w3_bf0 = round_w3(0, slot([P, wide], BF16, "words0")[:])
-        late = slot([P, 3 * wide], BF16, "H")
-
-        def weave(x):
-            grouped = late[:, x * wide : (x + 1) * wide]
-            nc.scalar.copy(
-                grouped.rearrange("p (c i t) -> p c t i", i=4, t=PACK),
-                planes[:, x].rearrange("p t (c i) -> p c t i", i=4),
+        w3_q = [quantise(weave(held([P, WIDE], BF16, "words0")[:], w3_raw[0], 2), "w3q0", 1)]
+        apart_bf0 = placed([P, WIDE], BF16, "apart_bf0", APART_AT)
+        late = placed([P, 2 * WIDE], BF16, "late", LATE_AT)
+        apart = [quantise(weave(apart_bf0[:], planes0[:, 0], 1), "apart0", 1)]
+        joint = [quantise(weave(late[:, 0:WIDE], planes0[:, 1], 1), "joint0", 1)]
+        w3_bf1 = weave(late[:, WIDE : 2 * WIDE], w3_raw[1], 2)
+        joint_bf1 = weave(held([P, WIDE], BF16, "rows0")[:], sums1[:], 2)
+        apart_bf1 = placed([P, WIDE], BF16, "apart_bf1", APART_AT)
+        for u in range(2):
+            part = slice(u * HALF // LINE, (u + 1) * HALF // LINE)
+            nc.vector.tensor_tensor(
+                woven(apart_bf1[:])[:, part], planar(left[:])[:, part], planar(right[:])[:, part], ALU.subtract
             )
-            return grouped
-
-        apart = {1: quantise(combine(left, right, ALU.subtract, "E", 2), "apart1", 2)}
-        joint = {1: quantise(combine(left, right, ALU.add, "rows0", 2), "joint1", 2)}
-        w3_bf1 = round_w3(1, late[:, 2 * wide : 3 * wide])
-        w3_q = [quantise(w3_bf0, "w3q0", 1), quantise(w3_bf1, "w3q1", 1)]
-        apart[0] = quantise(weave(0), "apart0", 1)
-        joint[0] = quantise(weave(1), "joint0", 1)
+        apart.append(quantise(apart_bf1[:], "apart1", 2))
+        w3_q.append(quantise(w3_bf1, "w3q1", 1))
+        joint.append(quantise(joint_bf1, "joint1", 2))
 
         tiles = N // P
-        e_banks = [psum.tile([P, BANK], F32, name="bank") for c in range(tiles)]
-        f_banks = [psum.tile([P, BANK], F32, name="bank") for c in range(tiles)]
+        e_banks = new_banks(tiles)
+        f_banks = new_banks(tiles)
+
+        def second_pass(bank, b, w_codes, w_scales, moving):
+            nc.tensor.matmul_mx(
+                out=bank[:],
+                lhsT=w_codes,
+                lhsT_scale=w_scales,
+                rhs=moving[0][:].bitcast(FP8X4),
+                rhs_scale=moving[1][:],
+                start=(b == 0),
+                stop=(b == PASSES2 - 1),
+            )
 
         def e_pass(c, b):
-            codes, scales = apart[b]
-            nc.tensor.matmul_mx(
-                out=e_banks[c][:],
-                lhsT=w2_word[:, b, 2 * P * c : 2 * P * (c + 1)].bitcast(FP4X4),
-                lhsT_scale=w2_scale[:, b * N + P * c : b * N + P * (c + 1)],
-                rhs=codes[:].bitcast(FP8X4),
-                rhs_scale=scales[:],
-                start=(b == 1),
-                stop=(b == 0),
-            )
+            codes = w2_word[:, b, 2 * P * c : 2 * P * (c + 1)].bitcast(FP4X4)
+            second_pass(e_banks[c], b, codes, w2_scale[:, b * N + P * c : b * N + P * (c + 1)], apart[b])
 
         def f_pass(c, b):
-            codes, scales = joint[b]
-            w_codes, w_scales = w3_q[b]
-            nc.tensor.matmul_mx(
-                out=f_banks[c][:],
-                lhsT=w_codes[:, P * c : P * (c + 1)].bitcast(FP8X4),
-                lhsT_scale=w_scales[:, P * c : P * (c + 1)],
-                rhs=codes[:].bitcast(FP8X4),
-                rhs_scale=scales[:],
-                start=(b == 1),
-                stop=(b == 0),
-            )
+            codes, scales = w3_q[b]
+            cols = slice(P * c, P * (c + 1))
+            second_pass(f_banks[c], b, codes[:, cols].bitcast(FP8X4), scales[:, cols], joint[b])
 
         for c in range(tiles):
-            e_pass(c, 1)
-        for c in range(tiles):
-            f_pass(c, 1)
-        size = []
-        for c in range(tiles):
             e_pass(c, 0)
-            size.append(held([P, PAIRS], F32, "size%d" % c))
-            nc.scalar.activation(size[c][:], e_banks[c][:], ACT.Abs)
         for c in range(tiles):
             f_pass(c, 0)
+        size = [held([P, PAIRS], F32, "size%d" % c) for c in range(tiles)]
+        for c in range(tiles):
+            e_pass(c, 1)
+            nc.scalar.activation(size[c][:], e_banks[c][:], ACT.Abs)
+        for c in range(tiles):
+            f_pass(c, 1)
             result = held([P, PAIRS], F32, "result%d" % c)
             nc.vector.scalar_tensor_tensor(
                 result[:], f_banks[c][:], b3_sb[:, c : c + 1], size[c][:], ALU.add, ALU.max

from contextlib import ExitStack

import concourse.mybir as mybir

K, T, S, H, PAIRS, N = 1536, 4096, 1024, 1024, 512, 512
FLOPS = 2 * K * H * S + 2 * 2 * H * N * PAIRS

F32 = mybir.dt.float32
BF16 = mybir.dt.bfloat16
I32 = mybir.dt.int32
U32 = mybir.dt.uint32
U16 = mybir.dt.uint16
U8 = mybir.dt.uint8
FP8X4 = mybir.dt.float8_e4m3fn_x4
FP4X4 = mybir.dt.float4_e2m1fn_x4
ALU = mybir.AluOpType
ACT = mybir.ActivationFunctionType

P = 128
PACK = 4
K_PASS = P * PACK
BANK = 512
BANKS = 8
WIDE = PACK * K_PASS
HALF = K_PASS // 2
PASSES1 = K // K_PASS
PASSES2 = H // K_PASS
QUADS = 4
QUAD = P // QUADS
QUAD_ROWS = 4
LINE = 4
LIST_ROWS = 16
FIRST_ROW = QUAD - QUAD_ROWS * PASSES1
MOVED = (QUADS - 1) * QUAD + QUAD_ROWS

KB = 1024
WORDS2_AT, TAB_SCALE_AT, V_WORD0_AT, HALVES_AT = 0, 7 * KB, 8 * KB, 10 * KB
APART_AT, LAST_TANH_AT, LATE_AT = 18 * KB, 20 * KB, 22 * KB


def tile_list_bone_pair_separation_kernel(
    tc, tab_words, tab_scales, offs, pos1, pos2, w1, gain, w2_words, w2_scales, w3, b3, out
):
    nc = tc.nc
    with ExitStack() as ctx:
        keep = ctx.enter_context(tc.tile_pool(name="keep", bufs=1))
        ring = ctx.enter_context(tc.tile_pool(name="ring", bufs=PACK))
        shared = ctx.enter_context(tc.tile_pool(name="shared", bufs=1))
        psum = ctx.enter_context(tc.psum_pool(name="psum", bufs=BANKS))

        def held(shape, dtype, name):
            return keep.tile(shape, dtype, name=name, align_bytes=64)

        def placed(shape, dtype, name, offset):
            return shared.tile(shape, dtype, name=name, align_bytes=64, offset=offset)

        def new_banks(count):
            return [psum.tile([P, BANK], F32, name="bank") for i in range(count)]

        offs_sb = keep.tile([P, S // LIST_ROWS], U16, name="offs_sb")
        pos1_sb = keep.tile([P, PAIRS // LIST_ROWS], U16, name="pos1_sb")
        pos2_sb = keep.tile([P, PAIRS // LIST_ROWS], U16, name="pos2_sb")

        tab_scale = placed([P, T], U8, "tab_scale", TAB_SCALE_AT)
        for q in range(QUADS):
            engine = nc.vector if q % 2 else nc.gpsimd
            engine.memset(tab_scale[QUAD * q : QUAD * q + FIRST_ROW, :].bitcast(I32), 0)
        picked_scale = held([P, S], U8, "picked_scale")
        v_scale = [held([P, S], U8, "v_scale%d" % a) for a in range(PASSES1)]
        for a in range(PASSES1):
            nc.vector.memset(v_scale[a][:].bitcast(I32), 0)

        def load_w(raw, w, row0, col0, width):
            nc.sync.dma_start(
                raw, w[row0 : row0 + K_PASS, col0 : col0 + width].rearrange("(p j) c -> p j c", j=PACK)
            )
            return raw

        def load_chunk(tile, w, row0, col0):
            return [load_w(tile[:], w, row0, col0, K_PASS)]

        def load_halves(tile, w, row0, col0):
            return [load_w(tile[:, u], w, row0, col0 + u * HALF, HALF) for u in range(2)]

        def load_words(words, a):
            nc.sync.dma_start(words[:].bitcast(I32), tab_words[a].bitcast(I32))
            return words

        chunk_shape, halves_shape = [P, PACK, K_PASS], [P, 2, PACK, HALF]

        nc.sync.dma_start(offs_sb[:], offs)
        tab_word = [load_words(held([P, T], U16, "words0"), 0)]
        for q in range(QUADS):
            nc.sync.dma_start(
                tab_scale[QUAD * q + FIRST_ROW : QUAD * (q + 1), :].bitcast(I32),
                tab_scales[:, QUAD_ROWS * q : QUAD_ROWS * (q + 1), :].bitcast(I32),
            )
        w1_raw = {}
        w1_raw[0, 0] = load_chunk(held(chunk_shape, F32, "rows0"), w1, 0, 0)
        tab_word.append(load_words(held([P, T], U16, "words1"), 1))
        w1_raw[0, 1] = load_chunk(held(chunk_shape, F32, "rows1"), w1, K_PASS, 0)
        nc.sync.dma_start(pos1_sb[:], pos1)
        nc.sync.dma_start(pos2_sb[:], pos2)
        gain_sb = held([P, PASSES2, PACK], F32, "gain_sb")
        nc.gpsimd.dma_start(gain_sb[:], gain.rearrange("(b p t) -> p b t", p=P, t=PACK))

        nc.vector.tensor_copy(picked_scale[:], tab_scale[:].indirect(offs_sb[:]))

        def move_scales(a):
            row = FIRST_ROW + QUAD_ROWS * a
            nc.sync.dma_start(
                v_scale[a][0:MOVED, :].bitcast(I32), picked_scale[row : row + MOVED, :].bitcast(I32)
            )

        move_scales(0)
        tab_word.append(load_words(placed([P, T], U16, "words2", WORDS2_AT), 2))
        move_scales(1)
        w1_raw[0, 2] = load_halves(placed(halves_shape, F32, "halves", HALVES_AT), w1, 2 * K_PASS, 0)
        move_scales(2)

        v_word = [placed([P, S], U16, "v_word0", V_WORD0_AT)]
        v_word.extend(held([P, S], U16, "v_word%d" % a) for a in range(1, PASSES1))

        def quantise(rounded, name, pieces):
            codes = held([P, K_PASS], U32, name + "_codes")
            scales = held([P, K_PASS], U8, name + "_scales")
            w = K_PASS // pieces
            for i in range(pieces):
                nc.vector.quantize_mx(
                    out=codes[:, i * w : (i + 1) * w].bitcast(FP8X4),
                    scales=scales[:, i * w : (i + 1) * w],
                    in_=rounded[:, PACK * i * w : PACK * (i + 1) * w],
                )
            return codes, scales

        def round_w1(b, a, copies, rounded):
            dst = rounded.rearrange("p (t m j) -> p m j t", t=PACK, j=PACK)
            m = P // len(copies)
            for u, copy in enumerate(copies):
                copy(dst[:, u * m : (u + 1) * m], w1_raw[b, a][u].rearrange("p j (m t) -> p m j t", t=PACK))
            return rounded

        def woven(rounded):
            return rounded.rearrange("p (c i t) -> p c t i", i=LINE, t=PACK)

        def planar(planes):
            return planes.rearrange("p t (c i) -> p c t i", i=LINE)

        def weave(rounded, planes, pieces):
            c = K_PASS // LINE // pieces
            for u in range(pieces):
                nc.scalar.copy(woven(rounded)[:, u * c : (u + 1) * c], planar(planes)[:, u * c : (u + 1) * c])
            return rounded

        w1_q = {}

        def first_pass(banks, b, t, a, u):
            codes, scales = w1_q[b, a]
            nc.tensor.matmul_mx(
                out=banks[t][u][:],
                lhsT=codes[:, t * P : (t + 1) * P].bitcast(FP8X4),
                lhsT_scale=scales[:, t * P : (t + 1) * P],
                rhs=v_word[a][:, u * BANK : (u + 1) * BANK].bitcast(FP4X4),
                rhs_scale=v_scale[a][:, u * BANK : (u + 1) * BANK],
                start=(a == 0),
                stop=(a == PASSES1 - 1),
            )

        def first_stage(b, quantised_w1, ahead):
            banks = [new_banks(S // BANK) for t in range(PACK)]
            for a in range(PASSES1):
                w1_q[b, a] = quantised_w1(a)
                for t in range(PACK if a == 0 else ahead):
                    for u in range(S // BANK):
                        first_pass(banks, b, t, a, u)
            for t in range(ahead, PACK):
                for u in range(S // BANK):
                    for a in range(1, PASSES1):
                        first_pass(banks, b, t, a, u)
            return banks

        def gain_on_vector(h, tanh, g):
            for u in range(S // BANK):
                cols = slice(u * BANK, (u + 1) * BANK)
                nc.vector.tensor_scalar(h[:, cols], tanh[:, cols], g, None, ALU.mult)

        def gain_on_gpsimd(h, tanh, g):
            nc.gpsimd.tensor_scalar(h[:], tanh[:], g, 0.0, ALU.mult, ALU.add)

        def gain_on_scalar(h, tanh, g):
            nc.scalar.activation(h[:], tanh[:], ACT.Copy, scale=g)

        def make_slice(banks, b, t, tanh, apply_gain):
            for u in range(S // BANK):
                nc.scalar.activation(tanh[:, u * BANK : (u + 1) * BANK], banks[t][u][:], ACT.Tanh)
            h = ring.tile([P, S], F32, name="h", align_bytes=64)
            apply_gain(h, tanh, gain_sb[:, b, t : t + 1])
            return h

        def pick(h, left, right):
            nc.vector.tensor_copy(left, h[:].indirect(pos1_sb[:]))
            nc.vector.tensor_copy(right, h[:].indirect(pos2_sb[:]))

        def quantised_w1_low(a):
            nc.vector.tensor_copy(v_word[a][:], tab_word[a][:].indirect(offs_sb[:]))
            last = a == PASSES1 - 1
            copies = [nc.scalar.copy, nc.vector.tensor_copy] if last else [nc.scalar.copy]
            rounded = round_w1(0, a, copies, held([P, WIDE], BF16, "round%d" % a)[:])
            return quantise(rounded, "w1q0%d" % a, PACK if last else 1)

        banks0 = first_stage(0, quantised_w1_low, 2)

        w1_raw[1, 0] = load_halves(held(halves_shape, F32, "words1"), w1, 0, K_PASS)
        w1_raw[1, 1] = load_chunk(held(chunk_shape, F32, "rows1"), w1, K_PASS, K_PASS)
        w1_raw[1, 2] = load_chunk(placed(chunk_shape, F32, "rows12", WORDS2_AT), w1, 2 * K_PASS, K_PASS)

        h0 = [
            make_slice(banks0, 0, t, held([P, S], F32, "tanh%d" % t), gain_on_gpsimd if t else gain_on_vector)
            for t in range(PACK)
        ]
        pairs0 = [held([P, 2, PAIRS], F32, "pairs0%d" % t) for t in range(PACK - 1)]
        for t in range(PACK - 1):
            pick(h0[t], pairs0[t][:, 0], pairs0[t][:, 1])

        rounded1 = [held([P, WIDE], BF16, name)[:] for name in ["round0", "tanh0", "tanh1"]]

        def quantised_w1_high(a):
            copies = [nc.scalar.copy] if a else [nc.vector.tensor_copy, nc.vector.tensor_copy]
            return quantise(round_w1(1, a, copies, rounded1[a]), "w1q1%d" % a, 1)

        banks1 = first_stage(1, quantised_w1_high, 1)

        pairs0.append(held([P, 2, PAIRS], F32, "tanh1"))
        pick(h0[PACK - 1], pairs0[PACK - 1][:, 0], pairs0[PACK - 1][:, 1])
        planes0 = held([P, 2, PACK, PAIRS], BF16, "tanh3")
        for t in range(PACK):
            for x, op in enumerate([ALU.subtract, ALU.add]):
                nc.gpsimd.tensor_tensor(planes0[:, x, t], pairs0[t][:, 0], pairs0[t][:, 1], op)

        w2_word = held([P, PASSES2, 2 * N], U8, "round1")
        nc.sync.dma_start(w2_word[:].bitcast(I32), w2_words.rearrange("b p x -> p b x").bitcast(I32))
        b3_sb = held([P, N // P], F32, "words1")
        with nc.allow_non_contiguous_dma(reason="one bias value to a partition"):
            nc.sync.dma_start(b3_sb[:], b3.rearrange("(c p) -> p c", p=P))
        w2_scale = held([P, PASSES2 * N], U8, "round2")
        nc.gpsimd.memset(w2_scale[:].bitcast(I32), 0)
        for q in range(QUADS):
            nc.sync.dma_start(
                w2_scale[QUAD * q : QUAD * q + QUAD_ROWS, :].rearrange("r (b n) -> r b n", b=PASSES2).bitcast(I32),
                w2_scales[:, QUAD_ROWS * q : QUAD_ROWS * (q + 1), :].rearrange("b r n -> r b n").bitcast(I32),
            )
        w3_raw = [
            load_w(placed(chunk_shape, F32, "rows3%d" % b, at)[:], w3, b * K_PASS, 0, N)
            for b, at in enumerate([HALVES_AT, WORDS2_AT])
        ]

        left = held([P, PACK, PAIRS], F32, "left")
        right = held([P, PACK, PAIRS], F32, "right")
        sums1 = held([P, PACK, PAIRS], BF16, "sums1")
        tanh1 = [held([P, S], F32, name) for name in ["tanh0", "rows1", "tanh2"]]
        tanh1.append(placed([P, S], F32, "tanh13", LAST_TANH_AT))
        for t in range(PACK):
            h = make_slice(banks1, 1, t, tanh1[t], gain_on_scalar if t else gain_on_vector)
            pick(h, left[:, t], right[:, t])
            engine = nc.gpsimd if t < PACK - 1 else nc.vector
            engine.tensor_tensor(sums1[:, t], left[:, t], right[:, t], ALU.add)

        w3_q = [quantise(weave(held([P, WIDE], BF16, "words0")[:], w3_raw[0], 2), "w3q0", 1)]
        apart_bf0 = placed([P, WIDE], BF16, "apart_bf0", APART_AT)
        late = placed([P, 2 * WIDE], BF16, "late", LATE_AT)
        apart = [quantise(weave(apart_bf0[:], planes0[:, 0], 1), "apart0", 1)]
        joint = [quantise(weave(late[:, 0:WIDE], planes0[:, 1], 1), "joint0", 1)]
        w3_bf1 = weave(late[:, WIDE : 2 * WIDE], w3_raw[1], 2)
        joint_bf1 = weave(held([P, WIDE], BF16, "rows0")[:], sums1[:], 2)
        apart_bf1 = placed([P, WIDE], BF16, "apart_bf1", APART_AT)
        for u in range(2):
            part = slice(u * HALF // LINE, (u + 1) * HALF // LINE)
            nc.vector.tensor_tensor(
                woven(apart_bf1[:])[:, part], planar(left[:])[:, part], planar(right[:])[:, part], ALU.subtract
            )
        apart.append(quantise(apart_bf1[:], "apart1", 2))
        w3_q.append(quantise(w3_bf1, "w3q1", 1))
        joint.append(quantise(joint_bf1, "joint1", 2))

        tiles = N // P
        e_banks = new_banks(tiles)
        f_banks = new_banks(tiles)

        def second_pass(bank, b, w_codes, w_scales, moving):
            nc.tensor.matmul_mx(
                out=bank[:],
                lhsT=w_codes,
                lhsT_scale=w_scales,
                rhs=moving[0][:].bitcast(FP8X4),
                rhs_scale=moving[1][:],
                start=(b == 0),
                stop=(b == PASSES2 - 1),
            )

        def e_pass(c, b):
            codes = w2_word[:, b, 2 * P * c : 2 * P * (c + 1)].bitcast(FP4X4)
            second_pass(e_banks[c], b, codes, w2_scale[:, b * N + P * c : b * N + P * (c + 1)], apart[b])

        def f_pass(c, b):
            codes, scales = w3_q[b]
            cols = slice(P * c, P * (c + 1))
            second_pass(f_banks[c], b, codes[:, cols].bitcast(FP8X4), scales[:, cols], joint[b])

        for c in range(tiles):
            e_pass(c, 0)
        for c in range(tiles):
            f_pass(c, 0)
        size = [held([P, PAIRS], F32, "size%d" % c) for c in range(tiles)]
        for c in range(tiles):
            e_pass(c, 1)
            nc.scalar.activation(size[c][:], e_banks[c][:], ACT.Abs)
        for c in range(tiles):
            f_pass(c, 1)
            result = held([P, PAIRS], F32, "result%d" % c)
            nc.vector.scalar_tensor_tensor(
                result[:], f_banks[c][:], b3_sb[:, c : c + 1], size[c][:], ALU.add, ALU.max
            )
            nc.sync.dma_start(out[P * c : P * (c + 1), :], result[:])
